import numpy as np
import ml_dtypes


def mxq(x, axis, fmt="e4m3"):
    dtype, down = {"e4m3": (ml_dtypes.float8_e4m3fn, 7), "e5m2": (ml_dtypes.float8_e5m2, 14)}[fmt]
    v = np.moveaxis(np.asarray(x, np.float32).astype(ml_dtypes.bfloat16).astype(np.float64), axis, -1)
    blocks = v.reshape(v.shape[:-1] + (-1, 32))
    amax = np.abs(blocks).max(-1, keepdims=True)
    byte = np.maximum(np.where(amax > 0, np.frexp(amax)[1] - 1 + 127, 0) - down, 1)
    scale = np.exp2(byte - 127.0)
    codes = (blocks / scale).astype(np.float32).astype(dtype).astype(np.float64)
    return np.moveaxis((codes * scale).reshape(v.shape), -1, axis)


WIDE = False


def mx_kscale(k):
    if not WIDE:
        return np.ones(k)
    levels = np.array([10, -10, 5, -5, 0])
    if k % 512:
        return np.exp2(np.random.permutation(np.resize(levels, k // 32))).repeat(32)
    a = np.empty((k // 512, 16))
    for p in range(k // 512):
        a[p, :8] = np.random.permutation(np.resize(levels, 8))
        for g in range(8):
            far = levels[np.abs(levels - a[p, g]) >= 10]
            a[p, g + 8] = far[np.random.randint(len(far))]
    return np.exp2(a.ravel()).repeat(32)


def f64(x):
    return np.asarray(x).astype(np.float64)


def striped(idx):
    return np.tile(idx.reshape(-1, 16).T, (8, 1)).astype(np.uint16)


def unstriped(offs):
    return offs[:16].T.reshape(-1).astype(np.int64)


E2M1 = np.array([0.0, 0.5, 1.0, 1.5, 2.0, 3.0, 4.0, 6.0, -0.0, -0.5, -1.0, -1.5, -2.0, -3.0, -4.0, -6.0])


def pack_weight(w, fmt):
    k, n = w.shape
    w = f64(np.asarray(w, np.float32).astype(ml_dtypes.bfloat16)).reshape(k // 32, 32, n)
    amax = np.abs(w).max(1)
    if fmt == "e4m3":
        byte = np.frexp(amax)[1] - 1 + 127 - 7
    else:
        mant, ex = np.frexp(amax / 6.0)
        byte = np.where(mant > 0.5, ex, ex - 1) + 127
    byte = np.clip(np.where(amax > 0, byte, 1), 1, 254)
    scaled = (w * np.exp2(127.0 - byte)[:, None, :]).reshape(k, n).astype(np.float32)
    by_word = np.ascontiguousarray(scaled.reshape(k // 512, 128, 4, n).transpose(0, 1, 3, 2))
    if fmt == "e4m3":
        words = by_word.astype(ml_dtypes.float8_e4m3fn).view(np.uint8)
    else:
        c = by_word.astype(ml_dtypes.float4_e2m1fn).view(np.uint8) & 0xF
        words = (c[..., 0::2] | (c[..., 1::2] << 4)).reshape(k // 512, 128, 2 * n)
    return np.ascontiguousarray(words), np.ascontiguousarray(byte.astype(np.uint8).reshape(k // 512, 16, n))


def unpack_weight(words, scales, fmt):
    g, _, n = scales.shape
    words = np.ascontiguousarray(words).reshape(g, 128, n, -1)
    if fmt == "e4m3":
        vals = words.view(ml_dtypes.float8_e4m3fn).astype(np.float64)
    else:
        nib = np.empty((g, 128, n, 4), np.uint8)
        nib[..., 0::2] = words & 0xF
        nib[..., 1::2] = words >> 4
        vals = E2M1[nib]
    vals = vals * np.repeat(np.exp2(scales.astype(np.float64) - 127.0), 8, axis=1)[..., None]
    return vals.transpose(0, 1, 3, 2).reshape(g * 512, n)


def gelu(v):
    return 0.5 * v * (1.0 + np.tanh(np.sqrt(2.0 / np.pi) * (v + 0.044715 * v**3)))


K, T, E1, C1, E2, C2, H = 1024, 1024, 8, 128, 8, 128, 512
N = 256


def deal(E, C):
    slot_token = np.random.permutation(T)
    return slot_token, None, np.random.uniform(0.2, 1.0, T)


def by_expert(wq, xq, E, C):
    return np.concatenate([wq[e].T @ xq[:, e * C:(e + 1) * C] for e in range(E)], axis=1)


def setup_inputs():
    n = np.random.standard_normal
    s = mx_kscale(K)
    u = mx_kscale(H)
    slots1, pos1, g1 = deal(E1, C1)
    slots2, pos2, g2 = deal(E2, C2)
    x = pack_weight(n((K, T)) * s[:, None], "e4m3")
    w1 = [pack_weight(m, "e2m1") for m in n((E1, K, H)) / np.sqrt(K) / s[None, :, None] * u]
    return {
        "x_words": x[0],
        "x_scales": x[1],
        "w1_words": np.stack([m[0] for m in w1]),
        "w1_scales": np.stack([m[1] for m in w1]),
        "w2": (n((E2, H, N)) / np.sqrt(H) / u[None, :, None]).astype(np.float32),
        "gate1": (np.tile(g1, (128, 1))).astype(np.float32),
        "gate2": (np.tile(g2, (128, 1))).astype(np.float32),
        "offs": striped(slots1),
        "offs2": striped(slots2),
    }


def reference(x_words, x_scales, w1_words, w1_scales, w2, gate1, gate2, offs, offs2):
    w1 = np.stack([unpack_weight(w1_words[e], w1_scales[e], "e2m1") for e in range(E1)])
    w2q = mxq(f64(w2), 1, "e4m3")
    idx, idx2 = unstriped(offs), unstriped(offs2)
    xq = unpack_weight(x_words, x_scales, "e4m3")[:, idx]
    h = gelu(by_expert(w1, xq, E1, C1))
    c = np.zeros((H, T))
    c[:, idx] = f64(gate1[:1]) * h
    y = by_expert(w2q, mxq(c[:, idx2], 0, "e4m3"), E2, C2)
    out = np.zeros((N, T))
    out[:, idx2] = f64(gate2[:1]) * y
    return out

@@ -1,0 +1,226 @@
+from contextlib import ExitStack
+
+import concourse.mybir as mybir
+from concourse.masks import make_identity
+
+K, T, E, C, H, N = 1024, 1024, 8, 128, 512, 256
+FLOPS = 2 * T * (K * H + H * N)
+
+F32 = mybir.dt.float32
+BF16 = mybir.dt.bfloat16
+I32 = mybir.dt.int32
+U32 = mybir.dt.uint32
+U16 = mybir.dt.uint16
+U8 = mybir.dt.uint8
+FP8X4 = mybir.dt.float8_e4m3fn_x4
+FP4X4 = mybir.dt.float4_e2m1fn_x4
+ACT = mybir.ActivationFunctionType
+ALU = mybir.AluOpType
+
+P = 128
+CH = 256
+NCH = T // CH
+HALF = T // 2
+
+
+def tile_moe_ser_gelu_kernel(
+    tc, x_words, x_scales, w1_words, w1_scales, w2, gate1, gate2, offs, offs2, out
+):
+    nc = tc.nc
+    with ExitStack() as ctx:
+        keep = ctx.enter_context(tc.tile_pool(name="keep", bufs=1))
+        ring = ctx.enter_context(tc.tile_pool(name="ring", bufs=3))
+        psum = ctx.enter_context(tc.psum_pool(name="psum", bufs=2))
+        psum3 = ctx.enter_context(tc.psum_pool(name="psum3", bufs=3))
+
+        list1 = keep.tile([P, T // 16], U16, name="list1")
+        list2 = keep.tile([P, T // 16], U16, name="list2")
+
+        def entries(lst, first, count):
+            return lst[:, first // 16 : (first + count) // 16]
+
+        xw = [keep.tile([P, T], I32, name=f"xw{s}", align_bytes=64) for s in range(2)]
+        xs = keep.tile([P, 2, T], U8, name="xs", align_bytes=64)
+        w1s = keep.tile([P, 2 * E, H], U8, name="w1s", align_bytes=64)
+        w1w = [ring.tile([P, 4, 2 * H], U8, name=f"w1w{c}", tag="stream", align_bytes=64) for c in range(NCH)]
+        sg = [[keep.tile([P, HALF], U8, name=f"sg{h}_{s}", align_bytes=64) for s in range(2)] for h in range(2)]
+        grow = keep.tile([P, C], F32, name="grow")
+        gcol = keep.tile([P, E], F32, name="gcol")
+        ident = keep.tile([P, P], F32, name="ident")
+
+        nc.gpsimd.memset(xs[:].rearrange("p s t -> p (s t)").bitcast(I32), 0)
+        nc.vector.memset(w1s[:].rearrange("p a i -> p (a i)").bitcast(I32), 0)
+        nc.gpsimd.memset(grow[:], 0.0)
+        make_identity(nc, ident[:])
+
+        nc.sync.dma_start(list1[:], offs)
+        nc.sync.dma_start(xw[0][:], x_words[0].rearrange("p t d -> p (t d)").bitcast(I32))
+        for q in range(4):
+            nc.scalar.dma_start(
+                xs[32 * q : 32 * q + 4].bitcast(I32),
+                x_scales[:, 4 * q : 4 * q + 4, :].rearrange("s r t -> r s t").bitcast(I32),
+            )
+        nc.sync.dma_start(xw[1][:], x_words[1].rearrange("p t d -> p (t d)").bitcast(I32))
+        for q in range(4):
+            nc.scalar.dma_start(
+                w1s[32 * q : 32 * q + 4].bitcast(I32),
+                w1_scales[:, :, 4 * q : 4 * q + 4, :].rearrange("e s r i -> r (e s) i").bitcast(I32),
+            )
+        nc.sync.dma_start(grow[0:E, :], gate1[0].rearrange("(e c) -> e c", e=E))
+
+        def load_w1(c):
+            nc.sync.dma_start(
+                w1w[c][:].bitcast(I32),
+                w1_words[2 * c : 2 * c + 2].rearrange("e s p b -> p (e s) b").bitcast(I32),
+            )
+
+        load_w1(0)
+
+        gT = psum.tile([P, 4 * P], F32, name="gT", tag="tp")
+        nc.tensor.transpose(gT[:, 0:P], grow[:], ident[:])
+        nc.scalar.copy(gcol[:], gT[:, 0:E])
+
+        xg = [[keep.tile([P, CH], U32, name=f"xg{c}_{s}", align_bytes=64) for s in range(2)] for c in range(NCH)]
+
+        def gather_scales(h):
+            for s in range(2):
+                nc.vector.tensor_copy(sg[h][s][:], xs[:, s, :].indirect(entries(list1, h * HALF, HALF)))
+
+        def gather_words(c):
+            for s in range(2):
+                nc.vector.tensor_copy(xg[c][s][:], xw[s][:].bitcast(U32).indirect(entries(list1, c * CH, CH)))
+
+        gather_scales(0)
+        load_w1(1)
+        gather_words(0)
+        gather_words(1)
+        gather_scales(1)
+        for c in range(2, NCH):
+            load_w1(c)
+            gather_words(c)
+
+        nc.sync.dma_start(list2[:], offs2)
+
+        hg = keep.tile([P, E, H], F32, name="hg", tag="stage", align_bytes=64)
+        cs = keep.tile([P, 4, T], F32, name="cs")
+        for e in range(E):
+            c, el = divmod(e, 2)
+            acc = psum3.tile([P, H], F32, name="acc")
+            cols = slice(el * C, (el + 1) * C)
+            hcols = slice((e % 4) * C, (e % 4 + 1) * C)
+            for s in range(2):
+                nc.tensor.matmul_mx(
+                    acc[:],
+                    lhsT=xg[c][s][:, cols].bitcast(FP8X4),
+                    lhsT_scale=sg[e // 4][s][:, hcols],
+                    rhs=w1w[c][:, 2 * el + s, :].bitcast(FP4X4),
+                    rhs_scale=w1s[:, 2 * e + s, :],
+                    start=(s == 0),
+                    stop=(s == 1),
+                )
+            hh = ring.tile([P, 4, P], F32, name="hh")
+            nc.scalar.activation(hh[:], acc[:].rearrange("m (p t) -> m t p", t=4), ACT.Gelu_apprx_tanh)
+            nc.gpsimd.tensor_scalar(
+                hg[:, e, :], hh[:].rearrange("m t p -> m (t p)"), gcol[:, e : e + 1], 0.0, ALU.mult, ALU.add
+            )
+            tp = psum.tile([P, 4 * P], F32, name="tp", tag="tp")
+            for t in range(4):
+                nc.tensor.transpose(tp[:, t * P : (t + 1) * P], hg[:, e, t * P : (t + 1) * P], ident[:])
+            nc.scalar.copy(cs[:, :, e * C : (e + 1) * C], tp[:].rearrange("p (t m) -> p t m", t=4))
+
+        cw = [keep.tile([P, T], F32, name=f"cw{t}") for t in range(4)]
+        cb = [keep.tile([P, T], BF16, name=f"cb{t}") for t in range(4)]
+        ci = keep.tile([P, T, 4], BF16, name="ci", align_bytes=64)
+
+        def scatter_c(t, lo, hi):
+            nc.vector.tensor_copy(cw[t][:].indirect(entries(list1, lo, hi - lo)), cs[:, t, lo:hi])
+
+        def gather_c(t, lo, hi):
+            nc.scalar.activation(ci[:, lo:hi, t], cb[t][:].indirect(entries(list2, lo, hi - lo)), ACT.Copy)
+
+        for t in range(3):
+            scatter_c(t, 0, CH)
+        for c in range(1, NCH):
+            for t in range(2):
+                scatter_c(t, c * CH, (c + 1) * CH)
+        scatter_c(2, CH, T)
+        scatter_c(3, 0, CH)
+        scatter_c(3, CH, T)
+        nc.scalar.copy(cb[0][:], cw[0][:])
+        for t in (1, 2):
+            nc.gpsimd.tensor_scalar(cb[t][:], cw[t][:], 1.0, 0.0, ALU.mult, ALU.add)
+        nc.vector.tensor_copy(cb[3][:], cw[3][:])
+        for t in range(3):
+            for h in range(2):
+                gather_c(t, h * HALF, (h + 1) * HALF)
+
+        w2b = keep.tile([P, E, N, 4], BF16, name="w2b", tag="stage", align_bytes=64)
+        for e in range(E):
+            w2raw = ring.tile([P, 4, N], F32, name="w2raw", tag="stream", align_bytes=64)
+            nc.sync.dma_start(w2raw[:], w2[e].rearrange("(p j) n -> p j n", j=4))
+            nc.gpsimd.tensor_scalar(
+                w2b[:, e], w2raw[:].rearrange("p j n -> p n j"), 1.0, 0.0, ALU.mult, ALU.add
+            )
+        g2 = ring.tile([P, T], F32, name="g2", tag="stream", align_bytes=64)
+        nc.sync.dma_start(g2[:], gate2)
+
+        w2q = keep.tile([P, E * N], U32, name="w2q", align_bytes=64)
+        w2s = keep.tile([P, E * N], U8, name="w2s", align_bytes=64)
+        cq = keep.tile([P, T], U32, name="cq", align_bytes=64)
+        cqs = keep.tile([P, T], U8, name="cqs", align_bytes=64)
+        ys = keep.tile([P, 2, T], F32, name="ys")
+        ow = [keep.tile([P, T], F32, name=f"ow{j}") for j in range(2)]
+
+        def quantize_w2(c):
+            cols = slice(2 * c * N, 2 * (c + 1) * N)
+            nc.vector.quantize_mx(
+                w2q[:, cols].bitcast(FP8X4), w2s[:, cols], w2b[:, 2 * c : 2 * c + 2].rearrange("p e n j -> p (e n j)")
+            )
+
+        def layer2(lo, hi):
+            nc.vector.quantize_mx(
+                cq[:, lo:hi].bitcast(FP8X4), cqs[:, lo:hi], ci[:, lo:hi, :].rearrange("p m j -> p (m j)")
+            )
+            for g in range(lo, hi, CH):
+                w = min(CH, hi - g)
+                yb = psum.tile([P, 2, CH], F32, name="yb", tag="yb")
+                for m in range(g, g + w, C):
+                    e = m // C
+                    for j in range(2):
+                        ncols = slice(e * N + j * P, e * N + (j + 1) * P)
+                        nc.tensor.matmul_mx(
+                            yb[:, j, m - g : m - g + C],
+                            lhsT=w2q[:, ncols].bitcast(FP8X4),
+                            lhsT_scale=w2s[:, ncols],
+                            rhs=cq[:, m : m + C].bitcast(FP8X4),
+                            rhs_scale=cqs[:, m : m + C],
+                            start=True,
+                            stop=True,
+                        )
+                nc.scalar.copy(ys[:, :, g : g + w], yb[:, :, 0:w])
+
+        def scatter_y(lo, hi):
+            for j in range(2):
+                nc.vector.tensor_tensor(
+                    ow[j][:].indirect(entries(list2, lo, hi - lo)), ys[:, j, lo:hi], g2[:, lo:hi], ALU.mult
+                )
+
+        pieces = ((0, 128), (128, 256), (256, 512), (512, 1024))
+        gather_c(3, *pieces[0])
+        gather_c(3, *pieces[1])
+        quantize_w2(0)
+        layer2(*pieces[0])
+        gather_c(3, *pieces[2])
+        quantize_w2(1)
+        layer2(*pieces[1])
+        gather_c(3, *pieces[3])
+        quantize_w2(2)
+        quantize_w2(3)
+        scatter_y(*pieces[0])
+        layer2(*pieces[2])
+        scatter_y(*pieces[1])
+        layer2(*pieces[3])
+        scatter_y(*pieces[2])
+        scatter_y(*pieces[3])
+        for j in range(2):
+            nc.sync.dma_start(out[j * P : (j + 1) * P, :], ow[j][:])

@@ -29,142 +29,150 @@ def tile_moe_ser_gelu_kernel(
     nc = tc.nc
     with ExitStack() as ctx:
         keep = ctx.enter_context(tc.tile_pool(name="keep", bufs=1))
-        ring = ctx.enter_context(tc.tile_pool(name="ring", bufs=3))
+        stream = ctx.enter_context(tc.tile_pool(name="stream", bufs=4))
         psum = ctx.enter_context(tc.psum_pool(name="psum", bufs=2))
         psum3 = ctx.enter_context(tc.psum_pool(name="psum3", bufs=3))
 
         list1 = keep.tile([P, T // 16], U16, name="list1")
         list2 = keep.tile([P, T // 16], U16, name="list2")
 
-        def entries(lst, first, count):
-            return lst[:, first // 16 : (first + count) // 16]
+        def entries(lst, lo, hi):
+            return lst[:, lo // 16 : hi // 16]
 
-        xw = [keep.tile([P, T], I32, name=f"xw{s}", align_bytes=64) for s in range(2)]
+        def streamed(shape, dtype, name):
+            return stream.tile(shape, dtype, name=name, tag="stream", align_bytes=64)
+
+        w1w = [streamed([P, 4, 2 * H], U8, "w1w0")]
+        xw = [streamed([P, T], I32, f"xw{s}") for s in range(2)]
+        w1w += [streamed([P, 4, 2 * H], U8, "w1w1")]
+        w1w += [keep.tile([P, 4, 2 * H], U8, name=f"w1w{c}", align_bytes=64) for c in range(2, NCH)]
+        w2raw = [streamed([P, 4, N], F32, f"w2raw{e}") for e in range(E)]
+        g2 = streamed([P, T], F32, "g2")
+        cp = streamed([P, T, 2], BF16, "cp")
+        cb = [streamed([P, T], BF16, f"cb{t}") for t in (1, 0)][::-1]
         xs = keep.tile([P, 2, T], U8, name="xs", align_bytes=64)
         w1s = keep.tile([P, 2 * E, H], U8, name="w1s", align_bytes=64)
-        w1w = [ring.tile([P, 4, 2 * H], U8, name=f"w1w{c}", tag="stream", align_bytes=64) for c in range(NCH)]
-        sg = [[keep.tile([P, HALF], U8, name=f"sg{h}_{s}", align_bytes=64) for s in range(2)] for h in range(2)]
-        grow = keep.tile([P, C], F32, name="grow")
-        gcol = keep.tile([P, E], F32, name="gcol")
         ident = keep.tile([P, P], F32, name="ident")
+        g1 = keep.tile([P, T], F32, name="g1")
 
-        nc.gpsimd.memset(xs[:].rearrange("p s t -> p (s t)").bitcast(I32), 0)
+        nc.vector.memset(xs[:].rearrange("p s t -> p (s t)").bitcast(I32), 0)
         nc.vector.memset(w1s[:].rearrange("p a i -> p (a i)").bitcast(I32), 0)
-        nc.gpsimd.memset(grow[:], 0.0)
-        make_identity(nc, ident[:])
+
+        def load_x(queue, s):
+            queue.dma_start(xw[s][:], x_words[s].rearrange("p t d -> p (t d)").bitcast(I32))
+
+        def load_w1(queue, c):
+            queue.dma_start(
+                w1w[c][:].bitcast(I32),
+                w1_words[2 * c : 2 * c + 2].rearrange("e s p b -> p (e s) b").bitcast(I32),
+            )
 
         nc.sync.dma_start(list1[:], offs)
-        nc.sync.dma_start(xw[0][:], x_words[0].rearrange("p t d -> p (t d)").bitcast(I32))
+        nc.sync.dma_start(list2[:], offs2)
+        load_x(nc.sync, 0)
+        load_x(nc.sync, 1)
         for q in range(4):
             nc.scalar.dma_start(
                 xs[32 * q : 32 * q + 4].bitcast(I32),
                 x_scales[:, 4 * q : 4 * q + 4, :].rearrange("s r t -> r s t").bitcast(I32),
             )
-        nc.sync.dma_start(xw[1][:], x_words[1].rearrange("p t d -> p (t d)").bitcast(I32))
         for q in range(4):
             nc.scalar.dma_start(
                 w1s[32 * q : 32 * q + 4].bitcast(I32),
                 w1_scales[:, :, 4 * q : 4 * q + 4, :].rearrange("e s r i -> r (e s) i").bitcast(I32),
             )
-        nc.sync.dma_start(grow[0:E, :], gate1[0].rearrange("(e c) -> e c", e=E))
+        make_identity(nc, ident[:])
+        for c in range(NCH):
+            load_w1(nc.gpsimd, c)
+            if c == 1:
+                nc.gpsimd.dma_start(g1[:], gate1)
 
-        def load_w1(c):
-            nc.sync.dma_start(
-                w1w[c][:].bitcast(I32),
-                w1_words[2 * c : 2 * c + 2].rearrange("e s p b -> p (e s) b").bitcast(I32),
-            )
+        xg = keep.tile([P, 2, T], U32, name="xg", tag="words", align_bytes=64)
+        sg = [keep.tile([P, T], U8, name=f"sg{s}", align_bytes=64) for s in range(2)]
 
-        load_w1(0)
+        def gather_words(s, lo, hi):
+            nc.vector.tensor_copy(xg[:, s, lo:hi], xw[s][:].bitcast(U32).indirect(entries(list1, lo, hi)))
 
-        gT = psum.tile([P, 4 * P], F32, name="gT", tag="tp")
-        nc.tensor.transpose(gT[:, 0:P], grow[:], ident[:])
-        nc.scalar.copy(gcol[:], gT[:, 0:E])
+        def gather_scales(s, lo, hi):
+            nc.vector.tensor_copy(sg[s][:, lo:hi], xs[:, s, :].indirect(entries(list1, lo, hi)))
 
-        xg = [[keep.tile([P, CH], U32, name=f"xg{c}_{s}", align_bytes=64) for s in range(2)] for c in range(NCH)]
+        gather_words(0, 0, HALF)
+        gather_scales(0, 0, HALF)
+        gather_scales(1, 0, HALF)
+        gather_words(1, 0, CH)
+        gather_words(1, CH, HALF)
+        for s in range(2):
+            gather_words(s, HALF, T)
+        for s in range(2):
+            gather_scales(s, HALF, T)
 
-        def gather_scales(h):
-            for s in range(2):
-                nc.vector.tensor_copy(sg[h][s][:], xs[:, s, :].indirect(entries(list1, h * HALF, HALF)))
+        hh = keep.tile([P, E, 4, P], F32, name="hh")
+        early = keep.tile([P, 2, T], F32, name="early")
 
-        def gather_words(c):
-            for s in range(2):
-                nc.vector.tensor_copy(xg[c][s][:], xw[s][:].bitcast(U32).indirect(entries(list1, c * CH, CH)))
+        def turn(e, first, into):
+            tp = psum.tile([P, 2, P], F32, name="tp", tag=f"bank{first}")
+            for t in range(2):
+                nc.tensor.transpose(tp[:, t, :], hh[:, e, first + t, :], ident[:])
+            nc.scalar.copy(into[:, :, e * C : (e + 1) * C], tp[:])
 
-        gather_scales(0)
-        load_w1(1)
-        gather_words(0)
-        gather_words(1)
-        gather_scales(1)
-        for c in range(2, NCH):
-            load_w1(c)
-            gather_words(c)
-
-        nc.sync.dma_start(list2[:], offs2)
-
-        hg = keep.tile([P, E, H], F32, name="hg", tag="stage", align_bytes=64)
-        cs = keep.tile([P, 4, T], F32, name="cs")
         for e in range(E):
             c, el = divmod(e, 2)
             acc = psum3.tile([P, H], F32, name="acc")
-            cols = slice(el * C, (el + 1) * C)
-            hcols = slice((e % 4) * C, (e % 4 + 1) * C)
+            cols = slice(e * C, (e + 1) * C)
             for s in range(2):
                 nc.tensor.matmul_mx(
                     acc[:],
-                    lhsT=xg[c][s][:, cols].bitcast(FP8X4),
-                    lhsT_scale=sg[e // 4][s][:, hcols],
+                    lhsT=xg[:, s, cols].bitcast(FP8X4),
+                    lhsT_scale=sg[s][:, cols],
                     rhs=w1w[c][:, 2 * el + s, :].bitcast(FP4X4),
                     rhs_scale=w1s[:, 2 * e + s, :],
                     start=(s == 0),
                     stop=(s == 1),
                 )
-            hh = ring.tile([P, 4, P], F32, name="hh")
-            nc.scalar.activation(hh[:], acc[:].rearrange("m (p t) -> m t p", t=4), ACT.Gelu_apprx_tanh)
-            nc.gpsimd.tensor_scalar(
-                hg[:, e, :], hh[:].rearrange("m t p -> m (t p)"), gcol[:, e : e + 1], 0.0, ALU.mult, ALU.add
+            nc.scalar.activation(hh[:, e], acc[:].rearrange("m (p t) -> m t p", t=4), ACT.Gelu_apprx_tanh)
+            turn(e, 0, early)
+        late = keep.tile([P, 2, T], F32, name="late", tag="words", align_bytes=64)
+        for e in range(E):
+            turn(e, 2, late)
+
+        w2b = keep.tile([P, E, N, 4], BF16, name="w2b", align_bytes=64)
+        for e in range(E):
+            nc.sync.dma_start(w2raw[e][:], w2[e].rearrange("(p j) n -> p j n", j=4))
+            nc.scalar.copy(
+                w2b[:, e].rearrange("p (n i) j -> p n j i", i=4),
+                w2raw[e][:].rearrange("p j (n i) -> p n j i", i=4),
             )
-            tp = psum.tile([P, 4 * P], F32, name="tp", tag="tp")
-            for t in range(4):
-                nc.tensor.transpose(tp[:, t * P : (t + 1) * P], hg[:, e, t * P : (t + 1) * P], ident[:])
-            nc.scalar.copy(cs[:, :, e * C : (e + 1) * C], tp[:].rearrange("p (t m) -> p t m", t=4))
+
+        nc.sync.dma_start(g2[:], gate2)
 
         cw = [keep.tile([P, T], F32, name=f"cw{t}") for t in range(4)]
-        cb = [keep.tile([P, T], BF16, name=f"cb{t}") for t in range(4)]
         ci = keep.tile([P, T, 4], BF16, name="ci", align_bytes=64)
 
         def scatter_c(t, lo, hi):
-            nc.vector.tensor_copy(cw[t][:].indirect(entries(list1, lo, hi - lo)), cs[:, t, lo:hi])
+            nc.vector.tensor_tensor(
+                cw[t][:].indirect(entries(list1, lo, hi)), (early, late)[t // 2][:, t % 2, lo:hi], g1[:, lo:hi], ALU.mult
+            )
 
-        def gather_c(t, lo, hi):
-            nc.scalar.activation(ci[:, lo:hi, t], cb[t][:].indirect(entries(list2, lo, hi - lo)), ACT.Copy)
-
-        for t in range(3):
-            scatter_c(t, 0, CH)
-        for c in range(1, NCH):
+        for c in range(NCH):
             for t in range(2):
                 scatter_c(t, c * CH, (c + 1) * CH)
-        scatter_c(2, CH, T)
-        scatter_c(3, 0, CH)
-        scatter_c(3, CH, T)
-        nc.scalar.copy(cb[0][:], cw[0][:])
-        for t in (1, 2):
-            nc.gpsimd.tensor_scalar(cb[t][:], cw[t][:], 1.0, 0.0, ALU.mult, ALU.add)
-        nc.vector.tensor_copy(cb[3][:], cw[3][:])
-        for t in range(3):
-            for h in range(2):
-                gather_c(t, h * HALF, (h + 1) * HALF)
+        for lo, hi in ((0, HALF), (HALF, T)):
+            for t in (2, 3):
+                scatter_c(t, lo, hi)
+        for t in range(2):
+            nc.scalar.copy(cb[t][:], cw[t][:])
+            for lo, hi in ((0, HALF), (HALF, T)):
+                nc.scalar.activation(ci[:, lo:hi, t], cb[t][:].indirect(entries(list2, lo, hi)), ACT.Copy)
+        for t in (2, 3):
+            nc.scalar.copy(cp[:, :, t - 2], cw[t][:])
 
-        w2b = keep.tile([P, E, N, 4], BF16, name="w2b", tag="stage", align_bytes=64)
-        for e in range(E):
-            w2raw = ring.tile([P, 4, N], F32, name="w2raw", tag="stream", align_bytes=64)
-            nc.sync.dma_start(w2raw[:], w2[e].rearrange("(p j) n -> p j n", j=4))
-            nc.gpsimd.tensor_scalar(
-                w2b[:, e], w2raw[:].rearrange("p j n -> p n j"), 1.0, 0.0, ALU.mult, ALU.add
+        def gather_pairs(lo, hi):
+            nc.vector.tensor_copy(
+                ci[:].bitcast(U32)[:, lo:hi, 1],
+                cp[:].rearrange("p m d -> p (m d)").bitcast(U32).indirect(entries(list2, lo, hi)),
             )
-        g2 = ring.tile([P, T], F32, name="g2", tag="stream", align_bytes=64)
-        nc.sync.dma_start(g2[:], gate2)
 
-        w2q = keep.tile([P, E * N], U32, name="w2q", align_bytes=64)
+        w2q = keep.tile([P, E * N], U32, name="w2q", tag="words", align_bytes=64)
         w2s = keep.tile([P, E * N], U8, name="w2s", align_bytes=64)
         cq = keep.tile([P, T], U32, name="cq", align_bytes=64)
         cqs = keep.tile([P, T], U8, name="cqs", align_bytes=64)
@@ -183,7 +191,7 @@ def tile_moe_ser_gelu_kernel(
             )
             for g in range(lo, hi, CH):
                 w = min(CH, hi - g)
-                yb = psum.tile([P, 2, CH], F32, name="yb", tag="yb")
+                yb = psum.tile([P, 2, CH], F32, name="yb", tag="bank2")
                 for m in range(g, g + w, C):
                     e = m // C
                     for j in range(2):
@@ -202,25 +210,20 @@ def tile_moe_ser_gelu_kernel(
         def scatter_y(lo, hi):
             for j in range(2):
                 nc.vector.tensor_tensor(
-                    ow[j][:].indirect(entries(list2, lo, hi - lo)), ys[:, j, lo:hi], g2[:, lo:hi], ALU.mult
+                    ow[j][:].indirect(entries(list2, lo, hi)), ys[:, j, lo:hi], g2[:, lo:hi], ALU.mult
                 )
 
-        pieces = ((0, 128), (128, 256), (256, 512), (512, 1024))
-        gather_c(3, *pieces[0])
-        gather_c(3, *pieces[1])
-        quantize_w2(0)
-        layer2(*pieces[0])
-        gather_c(3, *pieces[2])
-        quantize_w2(1)
-        layer2(*pieces[1])
-        gather_c(3, *pieces[3])
-        quantize_w2(2)
-        quantize_w2(3)
+        for c in range(NCH):
+            quantize_w2(c)
+        pieces = ((0, CH), (CH, HALF), (HALF, T))
+        gather_pairs(*pieces[0])
+        for before, piece in zip(pieces, pieces[1:]):
+            gather_pairs(*piece)
+            layer2(*before)
         scatter_y(*pieces[0])
         layer2(*pieces[2])
         scatter_y(*pieces[1])
-        layer2(*pieces[3])
         scatter_y(*pieces[2])
-        scatter_y(*pieces[3])
+
         for j in range(2):
             nc.sync.dma_start(out[j * P : (j + 1) * P, :], ow[j][:])

@@ -47,15 +47,15 @@ def tile_moe_ser_gelu_kernel(
         w1w += [streamed([P, 4, 2 * H], U8, "w1w1")]
         w1w += [keep.tile([P, 4, 2 * H], U8, name=f"w1w{c}", align_bytes=64) for c in range(2, NCH)]
         w2raw = [streamed([P, 4, N], F32, f"w2raw{e}") for e in range(E)]
-        g2 = streamed([P, T], F32, "g2")
-        cp = streamed([P, T, 2], BF16, "cp")
         cb = [streamed([P, T], BF16, f"cb{t}") for t in (1, 0)][::-1]
-        xs = keep.tile([P, 2, T], U8, name="xs", align_bytes=64)
-        w1s = keep.tile([P, 2 * E, H], U8, name="w1s", align_bytes=64)
+        cp = streamed([P, T, 2], BF16, "cp")
+        g2 = streamed([P, T], F32, "g2")
+        xs = keep.tile([P, T], U8, name="xs", align_bytes=64)
+        w1s = keep.tile([P, 2 * E, H], U8, name="w1s", tag="weights", align_bytes=64)
         ident = keep.tile([P, P], F32, name="ident")
         g1 = keep.tile([P, T], F32, name="g1")
 
-        nc.vector.memset(xs[:].rearrange("p s t -> p (s t)").bitcast(I32), 0)
+        nc.vector.memset(xs[:].bitcast(I32), 0)
         nc.vector.memset(w1s[:].rearrange("p a i -> p (a i)").bitcast(I32), 0)
 
         def load_x(queue, s):
@@ -73,8 +73,7 @@ def tile_moe_ser_gelu_kernel(
         load_x(nc.sync, 1)
         for q in range(4):
             nc.scalar.dma_start(
-                xs[32 * q : 32 * q + 4].bitcast(I32),
-                x_scales[:, 4 * q : 4 * q + 4, :].rearrange("s r t -> r s t").bitcast(I32),
+                xs[32 * q : 32 * q + 8].bitcast(I32), x_scales[:, 4 * q : 4 * q + 4, :].bitcast(I32)
             )
         for q in range(4):
             nc.scalar.dma_start(
@@ -93,21 +92,20 @@ def tile_moe_ser_gelu_kernel(
         def gather_words(s, lo, hi):
             nc.vector.tensor_copy(xg[:, s, lo:hi], xw[s][:].bitcast(U32).indirect(entries(list1, lo, hi)))
 
-        def gather_scales(s, lo, hi):
-            nc.vector.tensor_copy(sg[s][:, lo:hi], xs[:, s, :].indirect(entries(list1, lo, hi)))
+        def gather_scales(lo, hi):
+            nc.vector.tensor_copy(sg[0][:, lo:hi], xs[:].indirect(entries(list1, lo, hi)))
+            nc.sync.dma_start(sg[1][0:112, lo:hi].bitcast(I32), sg[0][4:116, lo:hi].bitcast(I32))
 
-        gather_words(0, 0, HALF)
-        gather_scales(0, 0, HALF)
-        gather_scales(1, 0, HALF)
-        gather_words(1, 0, CH)
-        gather_words(1, CH, HALF)
+        nc.vector.memset(sg[1][:].bitcast(I32), 0)
+        for c, (lo, hi) in enumerate(((0, 3 * C), (3 * C, T))):
+            gather_scales(lo, hi)
+            for s in range(2):
+                gather_words(s, c * CH, (c + 1) * CH)
         for s in range(2):
             gather_words(s, HALF, T)
-        for s in range(2):
-            gather_scales(s, HALF, T)
 
         hh = keep.tile([P, E, 4, P], F32, name="hh")
-        early = keep.tile([P, 2, T], F32, name="early")
+        early = keep.tile([P, 2, T], F32, name="early", tag="early", align_bytes=64)
 
         def turn(e, first, into):
             tp = psum.tile([P, 2, P], F32, name="tp", tag=f"bank{first}")
@@ -135,15 +133,18 @@ def tile_moe_ser_gelu_kernel(
         for e in range(E):
             turn(e, 2, late)
 
-        w2b = keep.tile([P, E, N, 4], BF16, name="w2b", align_bytes=64)
-        for e in range(E):
+        w2b_most = keep.tile([P, E - 2, N, 4], BF16, name="w2b_most", tag="weights", align_bytes=64)
+        w2b_last = keep.tile([P, 2, N, 4], BF16, name="w2b_last", tag="early", align_bytes=64)
+        w2b = [w2b_most[:, 2 * c : 2 * c + 2] for c in range(NCH - 1)] + [w2b_last[:]]
+        def cast_w2(e, copy):
             nc.sync.dma_start(w2raw[e][:], w2[e].rearrange("(p j) n -> p j n", j=4))
-            nc.scalar.copy(
-                w2b[:, e].rearrange("p (n i) j -> p n j i", i=4),
+            copy(
+                w2b[e // 2][:, e % 2].rearrange("p (n i) j -> p n j i", i=4),
                 w2raw[e][:].rearrange("p j (n i) -> p n j i", i=4),
             )
 
-        nc.sync.dma_start(g2[:], gate2)
+        for e in range(E - 2):
+            cast_w2(e, nc.scalar.copy)
 
         cw = [keep.tile([P, T], F32, name=f"cw{t}") for t in range(4)]
         ci = keep.tile([P, T, 4], BF16, name="ci", align_bytes=64)
@@ -156,6 +157,9 @@ def tile_moe_ser_gelu_kernel(
         for c in range(NCH):
             for t in range(2):
                 scatter_c(t, c * CH, (c + 1) * CH)
+        for e in range(E - 2, E):
+            cast_w2(e, nc.vector.tensor_copy)
+        nc.sync.dma_start(g2[:], gate2)
         for lo, hi in ((0, HALF), (HALF, T)):
             for t in (2, 3):
                 scatter_c(t, lo, hi)
@@ -182,7 +186,7 @@ def tile_moe_ser_gelu_kernel(
         def quantize_w2(c):
             cols = slice(2 * c * N, 2 * (c + 1) * N)
             nc.vector.quantize_mx(
-                w2q[:, cols].bitcast(FP8X4), w2s[:, cols], w2b[:, 2 * c : 2 * c + 2].rearrange("p e n j -> p (e n j)")
+                w2q[:, cols].bitcast(FP8X4), w2s[:, cols], w2b[c].rearrange("p e n j -> p (e n j)")
             )
 
         def layer2(lo, hi):

@@ -18,9 +18,14 @@ ACT = mybir.ActivationFunctionType
 ALU = mybir.AluOpType
 
 P = 128
-CH = 256
+CH = 2 * C
 NCH = T // CH
 HALF = T // 2
+HALVES = ((0, HALF), (HALF, T))
+SHIFT = 4
+MOVED = 112
+LATE_W2 = (6, 7)
+MID_W2 = (4, 5)
 
 
 def tile_moe_ser_gelu_kernel(
@@ -46,9 +51,8 @@ def tile_moe_ser_gelu_kernel(
         xw = [streamed([P, T], I32, f"xw{s}") for s in range(2)]
         w1w += [streamed([P, 4, 2 * H], U8, "w1w1")]
         w1w += [keep.tile([P, 4, 2 * H], U8, name=f"w1w{c}", align_bytes=64) for c in range(2, NCH)]
-        w2raw = [streamed([P, 4, N], F32, f"w2raw{e}") for e in range(E)]
-        cb = [streamed([P, T], BF16, f"cb{t}") for t in (1, 0)][::-1]
-        cp = streamed([P, T, 2], BF16, "cp")
+        w2_streamed = {e: streamed([P, 4, N], F32, f"w2raw{e}") for e in range(E) if e not in MID_W2}
+        cp = keep.tile([P, T, 2], BF16, name="cp")
         g2 = streamed([P, T], F32, "g2")
         xs = keep.tile([P, T], U8, name="xs", align_bytes=64)
         w1s = keep.tile([P, 2 * E, H], U8, name="w1s", tag="weights", align_bytes=64)
@@ -58,22 +62,13 @@ def tile_moe_ser_gelu_kernel(
         nc.vector.memset(xs[:].bitcast(I32), 0)
         nc.vector.memset(w1s[:].rearrange("p a i -> p (a i)").bitcast(I32), 0)
 
-        def load_x(queue, s):
-            queue.dma_start(xw[s][:], x_words[s].rearrange("p t d -> p (t d)").bitcast(I32))
-
-        def load_w1(queue, c):
-            queue.dma_start(
-                w1w[c][:].bitcast(I32),
-                w1_words[2 * c : 2 * c + 2].rearrange("e s p b -> p (e s) b").bitcast(I32),
-            )
-
         nc.sync.dma_start(list1[:], offs)
         nc.sync.dma_start(list2[:], offs2)
-        load_x(nc.sync, 0)
-        load_x(nc.sync, 1)
+        for s in range(2):
+            nc.sync.dma_start(xw[s][:], x_words[s].rearrange("p t d -> p (t d)").bitcast(I32))
         for q in range(4):
             nc.scalar.dma_start(
-                xs[32 * q : 32 * q + 8].bitcast(I32), x_scales[:, 4 * q : 4 * q + 4, :].bitcast(I32)
+                xs[32 * q : 32 * q + 2 * SHIFT].bitcast(I32), x_scales[:, 4 * q : 4 * q + 4, :].bitcast(I32)
             )
         for q in range(4):
             nc.scalar.dma_start(
@@ -82,22 +77,30 @@ def tile_moe_ser_gelu_kernel(
             )
         make_identity(nc, ident[:])
         for c in range(NCH):
-            load_w1(nc.gpsimd, c)
+            nc.gpsimd.dma_start(
+                w1w[c][:].bitcast(I32),
+                w1_words[2 * c : 2 * c + 2].rearrange("e s p b -> p (e s) b").bitcast(I32),
+            )
             if c == 1:
                 nc.gpsimd.dma_start(g1[:], gate1)
 
         xg = keep.tile([P, 2, T], U32, name="xg", tag="words", align_bytes=64)
-        sg = [keep.tile([P, T], U8, name=f"sg{s}", align_bytes=64) for s in range(2)]
+        sg = [keep.tile([P, T], U8, name=f"sg{s}", tag=f"chain{s}", align_bytes=64) for s in range(2)]
+        w2mid = [keep.tile([P, 4, N], F32, name=f"w2mid{s}", tag=f"chain{s}", align_bytes=64) for s in range(2)]
+        cb = [keep.tile([P, T], BF16, name=f"cb{t}", tag=f"chain{1 - t}", align_bytes=64) for t in range(2)]
+        w2raw = [w2mid[e - MID_W2[0]] if e in MID_W2 else w2_streamed[e] for e in range(E)]
 
         def gather_words(s, lo, hi):
             nc.vector.tensor_copy(xg[:, s, lo:hi], xw[s][:].bitcast(U32).indirect(entries(list1, lo, hi)))
 
         def gather_scales(lo, hi):
             nc.vector.tensor_copy(sg[0][:, lo:hi], xs[:].indirect(entries(list1, lo, hi)))
-            nc.sync.dma_start(sg[1][0:112, lo:hi].bitcast(I32), sg[0][4:116, lo:hi].bitcast(I32))
+            nc.sync.dma_start(
+                sg[1][0:MOVED, lo:hi].bitcast(I32), sg[0][SHIFT : SHIFT + MOVED, lo:hi].bitcast(I32)
+            )
 
         nc.vector.memset(sg[1][:].bitcast(I32), 0)
-        for c, (lo, hi) in enumerate(((0, 3 * C), (3 * C, T))):
+        for c, (lo, hi) in enumerate(HALVES):
             gather_scales(lo, hi)
             for s in range(2):
                 gather_words(s, c * CH, (c + 1) * CH)
@@ -136,6 +139,7 @@ def tile_moe_ser_gelu_kernel(
         w2b_most = keep.tile([P, E - 2, N, 4], BF16, name="w2b_most", tag="weights", align_bytes=64)
         w2b_last = keep.tile([P, 2, N, 4], BF16, name="w2b_last", tag="early", align_bytes=64)
         w2b = [w2b_most[:, 2 * c : 2 * c + 2] for c in range(NCH - 1)] + [w2b_last[:]]
+
         def cast_w2(e, copy):
             nc.sync.dma_start(w2raw[e][:], w2[e].rearrange("(p j) n -> p j n", j=4))
             copy(
@@ -143,29 +147,28 @@ def tile_moe_ser_gelu_kernel(
                 w2raw[e][:].rearrange("p j (n i) -> p n j i", i=4),
             )
 
-        for e in range(E - 2):
+        for e in range(LATE_W2[0]):
             cast_w2(e, nc.scalar.copy)
 
         cw = [keep.tile([P, T], F32, name=f"cw{t}") for t in range(4)]
         ci = keep.tile([P, T, 4], BF16, name="ci", align_bytes=64)
 
         def scatter_c(t, lo, hi):
-            nc.vector.tensor_tensor(
-                cw[t][:].indirect(entries(list1, lo, hi)), (early, late)[t // 2][:, t % 2, lo:hi], g1[:, lo:hi], ALU.mult
-            )
+            values = (early, late)[t // 2][:, t % 2, lo:hi]
+            nc.vector.tensor_tensor(cw[t][:].indirect(entries(list1, lo, hi)), values, g1[:, lo:hi], ALU.mult)
 
-        for c in range(NCH):
+        for lo, hi in ((0, C), (C, CH), (CH, HALF), (HALF, HALF + CH), (HALF + CH, T)):
             for t in range(2):
-                scatter_c(t, c * CH, (c + 1) * CH)
-        for e in range(E - 2, E):
+                scatter_c(t, lo, hi)
+        for e in LATE_W2:
             cast_w2(e, nc.vector.tensor_copy)
         nc.sync.dma_start(g2[:], gate2)
-        for lo, hi in ((0, HALF), (HALF, T)):
+        for lo, hi in HALVES:
             for t in (2, 3):
                 scatter_c(t, lo, hi)
         for t in range(2):
             nc.scalar.copy(cb[t][:], cw[t][:])
-            for lo, hi in ((0, HALF), (HALF, T)):
+            for lo, hi in HALVES:
                 nc.scalar.activation(ci[:, lo:hi, t], cb[t][:].indirect(entries(list2, lo, hi)), ACT.Copy)
         for t in (2, 3):
             nc.scalar.copy(cp[:, :, t - 2], cw[t][:])
@@ -194,9 +197,8 @@ def tile_moe_ser_gelu_kernel(
                 cq[:, lo:hi].bitcast(FP8X4), cqs[:, lo:hi], ci[:, lo:hi, :].rearrange("p m j -> p (m j)")
             )
             for g in range(lo, hi, CH):
-                w = min(CH, hi - g)
                 yb = psum.tile([P, 2, CH], F32, name="yb", tag="bank2")
-                for m in range(g, g + w, C):
+                for m in range(g, g + CH, C):
                     e = m // C
                     for j in range(2):
                         ncols = slice(e * N + j * P, e * N + (j + 1) * P)
@@ -209,7 +211,7 @@ def tile_moe_ser_gelu_kernel(
                             start=True,
                             stop=True,
                         )
-                nc.scalar.copy(ys[:, :, g : g + w], yb[:, :, 0:w])
+                nc.scalar.copy(ys[:, :, g : g + CH], yb[:])
 
         def scatter_y(lo, hi):
             for j in range(2):

from contextlib import ExitStack

import concourse.mybir as mybir
from concourse.masks import make_identity

K, T, E, C, H, N = 1024, 1024, 8, 128, 512, 256
FLOPS = 2 * T * (K * H + H * N)

F32 = mybir.dt.float32
BF16 = mybir.dt.bfloat16
I32 = mybir.dt.int32
U32 = mybir.dt.uint32
U16 = mybir.dt.uint16
U8 = mybir.dt.uint8
FP8X4 = mybir.dt.float8_e4m3fn_x4
FP4X4 = mybir.dt.float4_e2m1fn_x4
ACT = mybir.ActivationFunctionType
ALU = mybir.AluOpType

P = 128
CH = 2 * C
NCH = T // CH
HALF = T // 2
HALVES = ((0, HALF), (HALF, T))
SHIFT = 4
MOVED = 112
LATE_W2 = (6, 7)
MID_W2 = (4, 5)


def tile_moe_ser_gelu_kernel(
    tc, x_words, x_scales, w1_words, w1_scales, w2, gate1, gate2, offs, offs2, out
):
    nc = tc.nc
    with ExitStack() as ctx:
        keep = ctx.enter_context(tc.tile_pool(name="keep", bufs=1))
        stream = ctx.enter_context(tc.tile_pool(name="stream", bufs=4))
        psum = ctx.enter_context(tc.psum_pool(name="psum", bufs=2))
        psum3 = ctx.enter_context(tc.psum_pool(name="psum3", bufs=3))

        list1 = keep.tile([P, T // 16], U16, name="list1")
        list2 = keep.tile([P, T // 16], U16, name="list2")

        def entries(lst, lo, hi):
            return lst[:, lo // 16 : hi // 16]

        def streamed(shape, dtype, name):
            return stream.tile(shape, dtype, name=name, tag="stream", align_bytes=64)

        w1w = [streamed([P, 4, 2 * H], U8, "w1w0")]
        xw = [streamed([P, T], I32, f"xw{s}") for s in range(2)]
        w1w += [streamed([P, 4, 2 * H], U8, "w1w1")]
        w1w += [keep.tile([P, 4, 2 * H], U8, name=f"w1w{c}", align_bytes=64) for c in range(2, NCH)]
        w2_streamed = {e: streamed([P, 4, N], F32, f"w2raw{e}") for e in range(E) if e not in MID_W2}
        cp = keep.tile([P, T, 2], BF16, name="cp")
        g2 = streamed([P, T], F32, "g2")
        xs = keep.tile([P, T], U8, name="xs", align_bytes=64)
        w1s = keep.tile([P, 2 * E, H], U8, name="w1s", tag="weights", align_bytes=64)
        ident = keep.tile([P, P], F32, name="ident")
        g1 = keep.tile([P, T], F32, name="g1")

        nc.vector.memset(xs[:].bitcast(I32), 0)
        nc.vector.memset(w1s[:].rearrange("p a i -> p (a i)").bitcast(I32), 0)

        nc.sync.dma_start(list1[:], offs)
        nc.sync.dma_start(list2[:], offs2)
        for s in range(2):
            nc.sync.dma_start(xw[s][:], x_words[s].rearrange("p t d -> p (t d)").bitcast(I32))
        for q in range(4):
            nc.scalar.dma_start(
                xs[32 * q : 32 * q + 2 * SHIFT].bitcast(I32), x_scales[:, 4 * q : 4 * q + 4, :].bitcast(I32)
            )
        for q in range(4):
            nc.scalar.dma_start(
                w1s[32 * q : 32 * q + 4].bitcast(I32),
                w1_scales[:, :, 4 * q : 4 * q + 4, :].rearrange("e s r i -> r (e s) i").bitcast(I32),
            )
        make_identity(nc, ident[:])
        for c in range(NCH):
            nc.gpsimd.dma_start(
                w1w[c][:].bitcast(I32),
                w1_words[2 * c : 2 * c + 2].rearrange("e s p b -> p (e s) b").bitcast(I32),
            )
            if c == 1:
                nc.gpsimd.dma_start(g1[:], gate1)

        xg = keep.tile([P, 2, T], U32, name="xg", tag="words", align_bytes=64)
        sg = [keep.tile([P, T], U8, name=f"sg{s}", tag=f"chain{s}", align_bytes=64) for s in range(2)]
        w2mid = [keep.tile([P, 4, N], F32, name=f"w2mid{s}", tag=f"chain{s}", align_bytes=64) for s in range(2)]
        cb = [keep.tile([P, T], BF16, name=f"cb{t}", tag=f"chain{1 - t}", align_bytes=64) for t in range(2)]
        w2raw = [w2mid[e - MID_W2[0]] if e in MID_W2 else w2_streamed[e] for e in range(E)]

        def gather_words(s, lo, hi):
            nc.vector.tensor_copy(xg[:, s, lo:hi], xw[s][:].bitcast(U32).indirect(entries(list1, lo, hi)))

        def gather_scales(lo, hi):
            nc.vector.tensor_copy(sg[0][:, lo:hi], xs[:].indirect(entries(list1, lo, hi)))
            nc.sync.dma_start(
                sg[1][0:MOVED, lo:hi].bitcast(I32), sg[0][SHIFT : SHIFT + MOVED, lo:hi].bitcast(I32)
            )

        nc.vector.memset(sg[1][:].bitcast(I32), 0)
        for c, (lo, hi) in enumerate(HALVES):
            gather_scales(lo, hi)
            for s in range(2):
                gather_words(s, c * CH, (c + 1) * CH)
        for s in range(2):
            gather_words(s, HALF, T)

        hh = keep.tile([P, E, 4, P], F32, name="hh")
        early = keep.tile([P, 2, T], F32, name="early", tag="early", align_bytes=64)

        def turn(e, first, into):
            tp = psum.tile([P, 2, P], F32, name="tp", tag=f"bank{first}")
            for t in range(2):
                nc.tensor.transpose(tp[:, t, :], hh[:, e, first + t, :], ident[:])
            nc.scalar.copy(into[:, :, e * C : (e + 1) * C], tp[:])

        for e in range(E):
            c, el = divmod(e, 2)
            acc = psum3.tile([P, H], F32, name="acc")
            cols = slice(e * C, (e + 1) * C)
            for s in range(2):
                nc.tensor.matmul_mx(
                    acc[:],
                    lhsT=xg[:, s, cols].bitcast(FP8X4),
                    lhsT_scale=sg[s][:, cols],
                    rhs=w1w[c][:, 2 * el + s, :].bitcast(FP4X4),
                    rhs_scale=w1s[:, 2 * e + s, :],
                    start=(s == 0),
                    stop=(s == 1),
                )
            nc.scalar.activation(hh[:, e], acc[:].rearrange("m (p t) -> m t p", t=4), ACT.Gelu_apprx_tanh)
            turn(e, 0, early)
        late = keep.tile([P, 2, T], F32, name="late", tag="words", align_bytes=64)
        for e in range(E):
            turn(e, 2, late)

        w2b_most = keep.tile([P, E - 2, N, 4], BF16, name="w2b_most", tag="weights", align_bytes=64)
        w2b_last = keep.tile([P, 2, N, 4], BF16, name="w2b_last", tag="early", align_bytes=64)
        w2b = [w2b_most[:, 2 * c : 2 * c + 2] for c in range(NCH - 1)] + [w2b_last[:]]

        def cast_w2(e, copy):
            nc.sync.dma_start(w2raw[e][:], w2[e].rearrange("(p j) n -> p j n", j=4))
            copy(
                w2b[e // 2][:, e % 2].rearrange("p (n i) j -> p n j i", i=4),
                w2raw[e][:].rearrange("p j (n i) -> p n j i", i=4),
            )

        for e in range(LATE_W2[0]):
            cast_w2(e, nc.scalar.copy)

        cw = [keep.tile([P, T], F32, name=f"cw{t}") for t in range(4)]
        ci = keep.tile([P, T, 4], BF16, name="ci", align_bytes=64)

        def scatter_c(t, lo, hi):
            values = (early, late)[t // 2][:, t % 2, lo:hi]
            nc.vector.tensor_tensor(cw[t][:].indirect(entries(list1, lo, hi)), values, g1[:, lo:hi], ALU.mult)

        for lo, hi in ((0, C), (C, CH), (CH, HALF), (HALF, HALF + CH), (HALF + CH, T)):
            for t in range(2):
                scatter_c(t, lo, hi)
        for e in LATE_W2:
            cast_w2(e, nc.vector.tensor_copy)
        nc.sync.dma_start(g2[:], gate2)
        for lo, hi in HALVES:
            for t in (2, 3):
                scatter_c(t, lo, hi)
        for t in range(2):
            nc.scalar.copy(cb[t][:], cw[t][:])
            for lo, hi in HALVES:
                nc.scalar.activation(ci[:, lo:hi, t], cb[t][:].indirect(entries(list2, lo, hi)), ACT.Copy)
        for t in (2, 3):
            nc.scalar.copy(cp[:, :, t - 2], cw[t][:])

        def gather_pairs(lo, hi):
            nc.vector.tensor_copy(
                ci[:].bitcast(U32)[:, lo:hi, 1],
                cp[:].rearrange("p m d -> p (m d)").bitcast(U32).indirect(entries(list2, lo, hi)),
            )

        w2q = keep.tile([P, E * N], U32, name="w2q", tag="words", align_bytes=64)
        w2s = keep.tile([P, E * N], U8, name="w2s", align_bytes=64)
        cq = keep.tile([P, T], U32, name="cq", align_bytes=64)
        cqs = keep.tile([P, T], U8, name="cqs", align_bytes=64)
        ys = keep.tile([P, 2, T], F32, name="ys")
        ow = [keep.tile([P, T], F32, name=f"ow{j}") for j in range(2)]

        def quantize_w2(c):
            cols = slice(2 * c * N, 2 * (c + 1) * N)
            nc.vector.quantize_mx(
                w2q[:, cols].bitcast(FP8X4), w2s[:, cols], w2b[c].rearrange("p e n j -> p (e n j)")
            )

        def layer2(lo, hi):
            nc.vector.quantize_mx(
                cq[:, lo:hi].bitcast(FP8X4), cqs[:, lo:hi], ci[:, lo:hi, :].rearrange("p m j -> p (m j)")
            )
            for g in range(lo, hi, CH):
                yb = psum.tile([P, 2, CH], F32, name="yb", tag="bank2")
                for m in range(g, g + CH, C):
                    e = m // C
                    for j in range(2):
                        ncols = slice(e * N + j * P, e * N + (j + 1) * P)
                        nc.tensor.matmul_mx(
                            yb[:, j, m - g : m - g + C],
                            lhsT=w2q[:, ncols].bitcast(FP8X4),
                            lhsT_scale=w2s[:, ncols],
                            rhs=cq[:, m : m + C].bitcast(FP8X4),
                            rhs_scale=cqs[:, m : m + C],
                            start=True,
                            stop=True,
                        )
                nc.scalar.copy(ys[:, :, g : g + CH], yb[:])

        def scatter_y(lo, hi):
            for j in range(2):
                nc.vector.tensor_tensor(
                    ow[j][:].indirect(entries(list2, lo, hi)), ys[:, j, lo:hi], g2[:, lo:hi], ALU.mult
                )

        for c in range(NCH):
            quantize_w2(c)
        pieces = ((0, CH), (CH, HALF), (HALF, T))
        gather_pairs(*pieces[0])
        for before, piece in zip(pieces, pieces[1:]):
            gather_pairs(*piece)
            layer2(*before)
        scatter_y(*pieces[0])
        layer2(*pieces[2])
        scatter_y(*pieces[1])
        scatter_y(*pieces[2])

        for j in range(2):
            nc.sync.dma_start(out[j * P : (j + 1) * P, :], ow[j][:])
